import numpy as np, ml_dtypes
CORES = [56,61,80,85]
N = 4
DEG, TK, TIMES = 4, 128, 2
MASK = [[0,1,2,3],[0,1,2,3],[0,1,2,3],[0,1,2,3]]
def setup_inputs(rng):
    return {"x": rng.standard_normal((N, 128, TK), dtype=np.float32).astype(ml_dtypes.bfloat16), "w": (rng.standard_normal((N, 128, DEG * 128), dtype=np.float32) / np.float32(np.sqrt(128 * DEG / 2))).astype(ml_dtypes.bfloat16)}
def setup_inputs_big(rng):
    d = setup_inputs(rng)
    for k in ("x",): d[k] = (d[k].astype(np.float32) * 1048576.0).astype(d[k].dtype)
    return d
def setup_inputs_small(rng):
    d = setup_inputs(rng)
    for k in ("x",): d[k] = (d[k].astype(np.float32) * (1 / 1048576.0)).astype(d[k].dtype)
    return d
def setup_inputs_apart(rng):
    d = setup_inputs(rng)
    f = (10.0 ** rng.permutation(np.linspace(-1.5, 1.5, N))).astype(np.float32).reshape(N, 1, 1)
    for k in ("x",): d[k] = (d[k].astype(np.float32) * f).astype(d[k].dtype)
    return d
def reference(x, w):
    X, W = x.astype(np.float64), w.astype(np.float64)
    h = list(X)
    for _ in range(TIMES):
        h = [np.maximum(sum(W[r][:, 128 * i:128 * i + 128].T @ h[j] for i, j in enumerate(MASK[r])), 0.0) for r in range(N)]
    return {"y": np.stack(h).astype(ml_dtypes.bfloat16)}

@@ -1,0 +1,188 @@
+from concourse.bass import DstId, RemoteDMATransfer
+from concourse.mybir import AluOpType
+
+NR, TK, DEG = 4, 128, 4
+WC = TK * DEG
+
+SCRATCH = {
+    "xd": ("dram", [128, TK], "bfloat16"),
+    "wd": ("dram", [128, WC], "bfloat16"),
+    "xs": ("sbuf", [128, NR * TK], "bfloat16"),
+    "ws": ("sbuf", [128, NR * WC], "bfloat16"),
+    "hs": ("sbuf", [128, NR * TK], "bfloat16"),
+    "ys": ("sbuf", [128, TK], "bfloat16"),
+    "zero": ("sbuf", [128, TK], "float32"),
+    "p0": ("psum", [128, 512], "float32"),
+    "p1": ("psum", [128, 512], "float32"),
+    "p2": ("psum", [128, 512], "float32"),
+    "p3": ("psum", [128, 512], "float32"),
+    "p4": ("psum", [128, 512], "float32"),
+}
+SEMAPHORES = (["lx", "lw", "ox", "ow", "xa", "wa", "sent", "zs", "st", "m4", "v4"]
+              + ["ax%d" % j for j in range(NR)] + ["aw%d" % j for j in range(NR)]
+              + ["m%d" % j for j in range(NR)] + ["v%d" % j for j in range(NR)])
+
+NX = 2
+NW = 8
+NF = 8
+NN = 16
+
+
+def _pick(mask, n, skip=0):
+    bits = [1 << b for b in range(mask.bit_length()) if (mask >> b) & 1]
+    m = 0
+    for b in bits[skip:skip + n]:
+        m |= b
+    return m
+
+
+def _plan(T, topo):
+    cores = list(T.cores)
+    near, far, ports, jobs = {}, {}, {}, {}
+    for r, c in enumerate(cores):
+        near[r] = [s for s, d in enumerate(cores) if s != r and topo.chip(d) == topo.chip(c)]
+        f = [s for s, d in enumerate(cores) if topo.chip(d) != topo.chip(c)]
+        far[r] = sorted(f, key=lambda s: (topo.die(cores[s]) != topo.die(c), s))
+        own = [p for p in range(topo.CORES_PER_CHIP * topo.CHIPS)
+               if topo.chip(p) == topo.chip(c) and topo.die(p) == topo.die(c) and p not in cores
+               and all(topo.may_write(p, cores[s]) for s in f)]
+        ports[r] = []
+        for k, s in enumerate(far[r]):
+            p = own[k % len(own)]
+            if p not in jobs:
+                jobs[p] = (r, [])
+                ports[r].append(p)
+            jobs[p][1].append(s)
+    return cores, near, far, ports, jobs
+
+
+def _dst(topo, c):
+    rid, pid, _ = topo.addr(c)
+    return DstId(rid=rid, pnc=pid)
+
+
+def _forward(g, core, T, topo, cores, job):
+    r, dsts = job
+    sem = T.sem
+    sent = 0
+    for src, arrived, n_in, land, width, name in ((T.xd, sem.xa, NX, T.xs, TK, "ax%d"), (T.wd, sem.wa, NW, T.ws, WC, "aw%d")):
+        g.wait_ge(arrived, n_in)
+        for s in dsts:
+            rid, pid, _ = topo.addr(cores[s])
+            g.remote_dma(land[:, r * width:(r + 1) * width], src[:], sem[name % r], sem.sent, pid, rid,
+                         _pick(topo.mask(core, cores[s]), NF))
+            sent += NF
+    g.wait_ge(sem.sent, sent)
+
+
+def _rank(g, core, T, topo, r, cores, near, far, ports):
+    sem = T.sem
+    mask_tab = T.tables["MASK"]
+
+    def xs(j):
+        return T.xs[:, j * TK:(j + 1) * TK]
+
+    def wall(j):
+        return T.ws[:, j * WC:(j + 1) * WC]
+
+    def wt(j, i):
+        return T.ws[:, j * WC + i * TK:j * WC + (i + 1) * TK]
+
+    def hs(j):
+        return T.hs[:, j * TK:(j + 1) * TK]
+
+    g.sync.dma_start(T.xd[:], T.x[:]).then_inc(sem.lx, 16)
+    g.sync.dma_start(T.wd[:], T.w[:]).then_inc(sem.lw, 16)
+    g.scalar.wait_ge(sem.lx, 16)
+    g.scalar.dma_start(wall(r), T.w[:]).then_inc(sem.ow, 16)
+    g.scalar.dma_start(xs(r), T.x[:]).then_inc(sem.ox, 16)
+    g.vector.memset(T.zero[:], 0.0).then_inc(sem.zs, 1)
+
+    sent = 0
+    for src, loaded, n, arrived in ((T.xd, sem.lx, NX, sem.xa), (T.wd, sem.lw, NW, sem.wa)):
+        g.wait_ge(loaded, 16)
+        g.remote_dma_fused(
+            [RemoteDMATransfer(dst_ids=[_dst(topo, p)], dma_engine_mask=_pick(topo.mask(core, p), n, k * n),
+                               remote_sem=arrived, src=src[:], dst=src[:]) for k, p in enumerate(ports[r])],
+            local_sem=sem.sent)
+        sent += n * len(ports[r])
+    for s in near[r]:
+        rid, pid, _ = topo.addr(cores[s])
+        m = _pick(topo.mask(core, cores[s]), NN)
+        g.remote_dma(xs(r), T.xd[:], sem["ax%d" % r], sem.sent, pid, rid, m)
+        g.remote_dma(wall(r), T.wd[:], sem["aw%d" % r], sem.sent, pid, rid, m)
+        sent += 2 * NN
+    g.wait_ge(sem.sent, sent)
+
+    here = [r] + near[r]
+    order = here + far[r]
+    pos = {j: k for k, j in enumerate(order)}
+    waited = set()
+
+    def need(name, val):
+        if name not in waited:
+            waited.add(name)
+            g.tensor.wait_ge(sem[name], val)
+
+    def need_x(j):
+        if j == r:
+            need("ox", 16)
+        else:
+            need("ax%d" % j, NN if j in near[r] else NF)
+
+    def need_w(j):
+        if j == r:
+            need("ow", 16)
+        else:
+            need("aw%d" % j, NN if j in near[r] else NF)
+
+    done = {}
+
+    def mm(grp, bank, total, lhsT, rhs):
+        k = done.get(grp, 0)
+        done[grp] = k + 1
+        ins = g.tensor.matmul(bank[:, 0:TK], lhsT, rhs, k == 0, k + 1 == total)
+        if k + 1 == total:
+            ins.then_inc(sem["m%d" % grp], 1)
+
+    def first(j, srcs):
+        for i, s in sorted(enumerate(mask_tab[j]), key=lambda t: pos[t[1]]):
+            if s in srcs:
+                need_w(j)
+                need_x(s)
+                mm(j, T["p%d" % j], len(mask_tab[j]), wt(j, i), xs(s))
+
+    def second(srcs):
+        for i, s in sorted(enumerate(mask_tab[r]), key=lambda t: pos[t[1]]):
+            if s in srcs:
+                need("v%d" % s, 1)
+                mm(NR, T.p4, len(mask_tab[r]), wt(r, i), hs(s))
+
+    for j in here:
+        first(j, here)
+    for j in here:
+        first(j, far[r])
+    second(here)
+    for j in far[r]:
+        first(j, order)
+    second(far[r])
+
+    g.vector.wait_ge(sem.zs, 1)
+    for j in order:
+        g.vector.wait_ge(sem["m%d" % j], 1)
+        g.vector.tensor_tensor(hs(j), T["p%d" % j][:, 0:TK], T.zero[:], AluOpType.max).then_inc(sem["v%d" % j], 1)
+    g.vector.wait_ge(sem.m4, 1)
+    g.vector.tensor_tensor(T.ys[:], T.p4[:, 0:TK], T.zero[:], AluOpType.max).then_inc(sem.v4, 1)
+
+    g.sync.wait_ge(sem.v4, 1)
+    g.sync.dma_start(T.y[:], T.ys[:]).then_inc(sem.st, 16)
+    g.sync.wait_ge(sem.st, 16)
+
+
+def rank_program(g, core, T, topo):
+    cores, near, far, ports, jobs = _plan(T, topo)
+    r = T.rank_of(core)
+    if r is not None:
+        _rank(g, core, T, topo, r, cores, near, far, ports)
+    elif core in jobs:
+        _forward(g, core, T, topo, cores, jobs[core])

@@ -3,10 +3,13 @@ from concourse.mybir import AluOpType
 
 NR, TK, DEG = 4, 128, 4
 WC = TK * DEG
+HC = 352
+LOW_FIRST = True
 
 SCRATCH = {
     "xd": ("dram", [128, TK], "bfloat16"),
-    "wd": ("dram", [128, WC], "bfloat16"),
+    "wl": ("dram", [128, HC], "bfloat16"),
+    "wh": ("dram", [128, WC - HC], "bfloat16"),
     "xs": ("sbuf", [128, NR * TK], "bfloat16"),
     "ws": ("sbuf", [128, NR * WC], "bfloat16"),
     "hs": ("sbuf", [128, NR * TK], "bfloat16"),
@@ -18,12 +21,13 @@ SCRATCH = {
     "p3": ("psum", [128, 512], "float32"),
     "p4": ("psum", [128, 512], "float32"),
 }
-SEMAPHORES = (["lx", "lw", "ox", "ow", "xa", "wa", "sent", "zs", "st", "m4", "v4"]
+SEMAPHORES = (["lx", "ll", "lh", "ox", "ow", "xa", "la", "ha", "sent", "zs", "st", "m4", "v4"]
               + ["ax%d" % j for j in range(NR)] + ["aw%d" % j for j in range(NR)]
+              + ["al%d" % j for j in range(NR)] + ["ah%d" % j for j in range(NR)]
               + ["m%d" % j for j in range(NR)] + ["v%d" % j for j in range(NR)])
 
 NX = 2
-NW = 8
+NH = 4
 NF = 8
 NN = 16
 
@@ -38,22 +42,21 @@ def _pick(mask, n, skip=0):
 
 def _plan(T, topo):
     cores = list(T.cores)
-    near, far, ports, jobs = {}, {}, {}, {}
+    every = range(topo.CORES_PER_CHIP * topo.CHIPS)
+    near, far, pa, pc, jobs = {}, {}, {}, {}, {}
     for r, c in enumerate(cores):
         near[r] = [s for s, d in enumerate(cores) if s != r and topo.chip(d) == topo.chip(c)]
         f = [s for s, d in enumerate(cores) if topo.chip(d) != topo.chip(c)]
         far[r] = sorted(f, key=lambda s: (topo.die(cores[s]) != topo.die(c), s))
-        own = [p for p in range(topo.CORES_PER_CHIP * topo.CHIPS)
-               if topo.chip(p) == topo.chip(c) and topo.die(p) == topo.die(c) and p not in cores
+        fit = [p for p in every if topo.die(p) == topo.die(c) and p not in cores
                and all(topo.may_write(p, cores[s]) for s in f)]
-        ports[r] = []
+        pa[r] = [p for p in fit if topo.chip(p) == topo.chip(c)][:len(f)]
+        pc[r] = [p for p in fit if topo.same_plane(topo.chip(p), topo.chip(c)) and topo.may_write(c, p)
+                 and all(topo.mates(topo.chip(p), topo.chip(cores[s])) for s in f)][:len(f)]
         for k, s in enumerate(far[r]):
-            p = own[k % len(own)]
-            if p not in jobs:
-                jobs[p] = (r, [])
-                ports[r].append(p)
-            jobs[p][1].append(s)
-    return cores, near, far, ports, jobs
+            jobs[pa[r][k]] = ("a", r, s)
+            jobs[pc[r][k]] = ("c", r, s)
+    return cores, near, far, pa, pc, jobs
 
 
 def _dst(topo, c):
@@ -62,20 +65,23 @@ def _dst(topo, c):
 
 
 def _forward(g, core, T, topo, cores, job):
-    r, dsts = job
+    way, r, s = job
     sem = T.sem
-    sent = 0
-    for src, arrived, n_in, land, width, name in ((T.xd, sem.xa, NX, T.xs, TK, "ax%d"), (T.wd, sem.wa, NW, T.ws, WC, "aw%d")):
-        g.wait_ge(arrived, n_in)
-        for s in dsts:
-            rid, pid, _ = topo.addr(cores[s])
-            g.remote_dma(land[:, r * width:(r + 1) * width], src[:], sem[name % r], sem.sent, pid, rid,
-                         _pick(topo.mask(core, cores[s]), NF))
-            sent += NF
-    g.wait_ge(sem.sent, sent)
+    rid, pid, _ = topo.addr(cores[s])
+    m = _pick(topo.mask(core, cores[s]), NF)
+    if way == "a":
+        g.wait_ge(sem.xa, NX)
+        g.remote_dma(T.xs[:, r * TK:(r + 1) * TK], T.xd[:], sem["ax%d" % r], sem.sent, pid, rid, m)
+        g.wait_ge(sem.la, NH)
+        g.remote_dma(T.ws[:, r * WC:r * WC + HC], T.wl[:], sem["al%d" % r], sem.sent, pid, rid, m)
+        g.wait_ge(sem.sent, 2 * NF)
+    else:
+        g.wait_ge(sem.ha, NH)
+        g.remote_dma(T.ws[:, r * WC + HC:(r + 1) * WC], T.wh[:], sem["ah%d" % r], sem.sent, pid, rid, m)
+        g.wait_ge(sem.sent, NF)
 
 
-def _rank(g, core, T, topo, r, cores, near, far, ports):
+def _rank(g, core, T, topo, r, cores, near, far, pa, pc):
     sem = T.sem
     mask_tab = T.tables["MASK"]
 
@@ -92,25 +98,35 @@ def _rank(g, core, T, topo, r, cores, near, far, ports):
         return T.hs[:, j * TK:(j + 1) * TK]
 
     g.sync.dma_start(T.xd[:], T.x[:]).then_inc(sem.lx, 16)
-    g.sync.dma_start(T.wd[:], T.w[:]).then_inc(sem.lw, 16)
-    g.scalar.wait_ge(sem.lx, 16)
+    g.sync.dma_start(T.wh[:], T.w[:, HC:WC]).then_inc(sem.lh, 16)
+    g.scalar.dma_start(T.wl[:], T.w[:, 0:HC]).then_inc(sem.ll, 16)
     g.scalar.dma_start(wall(r), T.w[:]).then_inc(sem.ow, 16)
     g.scalar.dma_start(xs(r), T.x[:]).then_inc(sem.ox, 16)
     g.vector.memset(T.zero[:], 0.0).then_inc(sem.zs, 1)
 
-    sent = 0
-    for src, loaded, n, arrived in ((T.xd, sem.lx, NX, sem.xa), (T.wd, sem.lw, NW, sem.wa)):
-        g.wait_ge(loaded, 16)
+    out = topo.mask(core, pc[r][0])
+    stay = topo.mask(core, pa[r][0]) & ~out
+
+    def spread(src, ports, engines, n, arrived):
         g.remote_dma_fused(
-            [RemoteDMATransfer(dst_ids=[_dst(topo, p)], dma_engine_mask=_pick(topo.mask(core, p), n, k * n),
-                               remote_sem=arrived, src=src[:], dst=src[:]) for k, p in enumerate(ports[r])],
+            [RemoteDMATransfer(dst_ids=[_dst(topo, p)], dma_engine_mask=_pick(engines, n, k * n),
+                               remote_sem=arrived, src=src[:], dst=src[:]) for k, p in enumerate(ports)],
             local_sem=sem.sent)
-        sent += n * len(ports[r])
+        return n * len(ports)
+
+    g.wait_ge(sem.lx, 16)
+    sent = spread(T.xd, pa[r], stay, NX, sem.xa)
+    g.wait_ge(sem.lh, 16)
+    sent += spread(T.wh, pc[r], out, NH, sem.ha)
+    g.wait_ge(sem.ll, 16)
+    sent += spread(T.wl, pa[r], stay, NH, sem.la)
+    g.wait_ge(sem.ox, 16)
+    g.wait_ge(sem.ow, 16)
     for s in near[r]:
         rid, pid, _ = topo.addr(cores[s])
         m = _pick(topo.mask(core, cores[s]), NN)
-        g.remote_dma(xs(r), T.xd[:], sem["ax%d" % r], sem.sent, pid, rid, m)
-        g.remote_dma(wall(r), T.wd[:], sem["aw%d" % r], sem.sent, pid, rid, m)
+        g.remote_dma(xs(r), xs(r), sem["ax%d" % r], sem.sent, pid, rid, m)
+        g.remote_dma(wall(r), wall(r), sem["aw%d" % r], sem.sent, pid, rid, m)
         sent += 2 * NN
     g.wait_ge(sem.sent, sent)
 
@@ -130,11 +146,16 @@ def _rank(g, core, T, topo, r, cores, near, far, ports):
         else:
             need("ax%d" % j, NN if j in near[r] else NF)
 
-    def need_w(j):
+    def need_w(j, i):
         if j == r:
             need("ow", 16)
+        elif j in near[r]:
+            need("aw%d" % j, NN)
         else:
-            need("aw%d" % j, NN if j in near[r] else NF)
+            if i * TK < HC:
+                need("al%d" % j, NF)
+            if (i + 1) * TK > HC:
+                need("ah%d" % j, NF)
 
     done = {}
 
@@ -145,10 +166,10 @@ def _rank(g, core, T, topo, r, cores, near, far, ports):
         if k + 1 == total:
             ins.then_inc(sem["m%d" % grp], 1)
 
-    def first(j, srcs):
+    def first(j, srcs, tiles):
         for i, s in sorted(enumerate(mask_tab[j]), key=lambda t: pos[t[1]]):
-            if s in srcs:
-                need_w(j)
+            if s in srcs and i in tiles:
+                need_w(j, i)
                 need_x(s)
                 mm(j, T["p%d" % j], len(mask_tab[j]), wt(j, i), xs(s))
 
@@ -158,13 +179,17 @@ def _rank(g, core, T, topo, r, cores, near, far, ports):
                 need("v%d" % s, 1)
                 mm(NR, T.p4, len(mask_tab[r]), wt(r, i), hs(s))
 
+    tiles = list(range(DEG))
+    low = [i for i in tiles if (i + 1) * TK <= HC]
+    high = [i for i in tiles if (i + 1) * TK > HC]
     for j in here:
-        first(j, here)
+        first(j, here, tiles)
     for j in here:
-        first(j, far[r])
+        first(j, far[r], tiles)
     second(here)
-    for j in far[r]:
-        first(j, order)
+    for part in ((low, high) if LOW_FIRST else (high, low)):
+        for j in far[r]:
+            first(j, order, part)
     second(far[r])
 
     g.vector.wait_ge(sem.zs, 1)
@@ -180,9 +205,9 @@ def _rank(g, core, T, topo, r, cores, near, far, ports):
 
 
 def rank_program(g, core, T, topo):
-    cores, near, far, ports, jobs = _plan(T, topo)
+    cores, near, far, pa, pc, jobs = _plan(T, topo)
     r = T.rank_of(core)
     if r is not None:
-        _rank(g, core, T, topo, r, cores, near, far, ports)
+        _rank(g, core, T, topo, r, cores, near, far, pa, pc)
     elif core in jobs:
         _forward(g, core, T, topo, cores, jobs[core])

@@ -3,11 +3,12 @@ from concourse.mybir import AluOpType
 
 NR, TK, DEG = 4, 128, 4
 WC = TK * DEG
-HC = 352
-LOW_FIRST = True
+XH = TK // 2
+HC = WC // 2
 
 SCRATCH = {
-    "xd": ("dram", [128, TK], "bfloat16"),
+    "x0": ("dram", [128, XH], "bfloat16"),
+    "x1": ("dram", [128, TK - XH], "bfloat16"),
     "wl": ("dram", [128, HC], "bfloat16"),
     "wh": ("dram", [128, WC - HC], "bfloat16"),
     "xs": ("sbuf", [128, NR * TK], "bfloat16"),
@@ -21,7 +22,7 @@ SCRATCH = {
     "p3": ("psum", [128, 512], "float32"),
     "p4": ("psum", [128, 512], "float32"),
 }
-SEMAPHORES = (["lx", "ll", "lh", "ox", "ow", "xa", "la", "ha", "sent", "zs", "st", "m4", "v4"]
+SEMAPHORES = (["lx", "lw", "ox", "ow", "xa", "wa", "sent", "zs", "st", "m4", "v4"]
               + ["ax%d" % j for j in range(NR)] + ["aw%d" % j for j in range(NR)]
               + ["al%d" % j for j in range(NR)] + ["ah%d" % j for j in range(NR)]
               + ["m%d" % j for j in range(NR)] + ["v%d" % j for j in range(NR)])
@@ -32,10 +33,10 @@ NF = 8
 NN = 16
 
 
-def _pick(mask, n, skip=0):
+def _pick(mask, n, skip=0, step=1):
     bits = [1 << b for b in range(mask.bit_length()) if (mask >> b) & 1]
     m = 0
-    for b in bits[skip:skip + n]:
+    for b in bits[skip:skip + n * step:step]:
         m |= b
     return m
 
@@ -69,16 +70,16 @@ def _forward(g, core, T, topo, cores, job):
     sem = T.sem
     rid, pid, _ = topo.addr(cores[s])
     m = _pick(topo.mask(core, cores[s]), NF)
+    g.wait_ge(sem.xa, NX)
     if way == "a":
-        g.wait_ge(sem.xa, NX)
-        g.remote_dma(T.xs[:, r * TK:(r + 1) * TK], T.xd[:], sem["ax%d" % r], sem.sent, pid, rid, m)
-        g.wait_ge(sem.la, NH)
+        g.remote_dma(T.xs[:, r * TK:r * TK + XH], T.x0[:], sem["ax%d" % r], sem.sent, pid, rid, m)
+        g.wait_ge(sem.wa, NH)
         g.remote_dma(T.ws[:, r * WC:r * WC + HC], T.wl[:], sem["al%d" % r], sem.sent, pid, rid, m)
-        g.wait_ge(sem.sent, 2 * NF)
     else:
-        g.wait_ge(sem.ha, NH)
+        g.remote_dma(T.xs[:, r * TK + XH:(r + 1) * TK], T.x1[:], sem["ax%d" % r], sem.sent, pid, rid, m)
+        g.wait_ge(sem.wa, NH)
         g.remote_dma(T.ws[:, r * WC + HC:(r + 1) * WC], T.wh[:], sem["ah%d" % r], sem.sent, pid, rid, m)
-        g.wait_ge(sem.sent, NF)
+    g.wait_ge(sem.sent, 2 * NF)
 
 
 def _rank(g, core, T, topo, r, cores, near, far, pa, pc):
@@ -97,29 +98,30 @@ def _rank(g, core, T, topo, r, cores, near, far, pa, pc):
     def hs(j):
         return T.hs[:, j * TK:(j + 1) * TK]
 
-    g.sync.dma_start(T.xd[:], T.x[:]).then_inc(sem.lx, 16)
-    g.sync.dma_start(T.wh[:], T.w[:, HC:WC]).then_inc(sem.lh, 16)
-    g.scalar.dma_start(T.wl[:], T.w[:, 0:HC]).then_inc(sem.ll, 16)
-    g.scalar.dma_start(wall(r), T.w[:]).then_inc(sem.ow, 16)
+    g.sync.dma_start(T.x0[:], T.x[:, 0:XH]).then_inc(sem.lx, 16)
+    g.scalar.dma_start(T.x1[:], T.x[:, XH:TK]).then_inc(sem.lx, 16)
+    g.sync.dma_start(T.wh[:], T.w[:, HC:WC]).then_inc(sem.lw, 16)
+    g.scalar.dma_start(T.wl[:], T.w[:, 0:HC]).then_inc(sem.lw, 16)
+    g.sync.dma_start(wall(r), T.w[:]).then_inc(sem.ow, 16)
     g.scalar.dma_start(xs(r), T.x[:]).then_inc(sem.ox, 16)
     g.vector.memset(T.zero[:], 0.0).then_inc(sem.zs, 1)
 
     out = topo.mask(core, pc[r][0])
     stay = topo.mask(core, pa[r][0]) & ~out
 
-    def spread(src, ports, engines, n, arrived):
+    def spread(jobs):
         g.remote_dma_fused(
-            [RemoteDMATransfer(dst_ids=[_dst(topo, p)], dma_engine_mask=_pick(engines, n, k * n),
-                               remote_sem=arrived, src=src[:], dst=src[:]) for k, p in enumerate(ports)],
+            [RemoteDMATransfer(dst_ids=[_dst(topo, p)], dma_engine_mask=m, remote_sem=arrived, src=src[:], dst=src[:])
+             for src, p, m, arrived in jobs],
             local_sem=sem.sent)
-        return n * len(ports)
+        return sum(bin(m).count("1") for _, _, m, _ in jobs)
 
-    g.wait_ge(sem.lx, 16)
-    sent = spread(T.xd, pa[r], stay, NX, sem.xa)
-    g.wait_ge(sem.lh, 16)
-    sent += spread(T.wh, pc[r], out, NH, sem.ha)
-    g.wait_ge(sem.ll, 16)
-    sent += spread(T.wl, pa[r], stay, NH, sem.la)
+    g.wait_ge(sem.lx, 32)
+    sent = spread([(T.x1, p, _pick(out, NX, k * NH, NH // NX), sem.xa) for k, p in enumerate(pc[r])]
+                  + [(T.x0, p, _pick(stay, NX, k * NH), sem.xa) for k, p in enumerate(pa[r])])
+    g.wait_ge(sem.lw, 32)
+    sent += spread([(T.wh, p, _pick(out, NH, k * NH), sem.wa) for k, p in enumerate(pc[r])]
+                   + [(T.wl, p, _pick(stay, NH, k * NH), sem.wa) for k, p in enumerate(pa[r])])
     g.wait_ge(sem.ox, 16)
     g.wait_ge(sem.ow, 16)
     for s in near[r]:
@@ -144,7 +146,7 @@ def _rank(g, core, T, topo, r, cores, near, far, pa, pc):
         if j == r:
             need("ox", 16)
         else:
-            need("ax%d" % j, NN if j in near[r] else NF)
+            need("ax%d" % j, NN if j in near[r] else 2 * NF)
 
     def need_w(j, i):
         if j == r:
@@ -186,11 +188,10 @@ def _rank(g, core, T, topo, r, cores, near, far, pa, pc):
         first(j, here, tiles)
     for j in here:
         first(j, far[r], tiles)
-    second(here)
-    for part in ((low, high) if LOW_FIRST else (high, low)):
+    for part in (low, high):
         for j in far[r]:
             first(j, order, part)
-    second(far[r])
+    second(order)
 
     g.vector.wait_ge(sem.zs, 1)
     for j in order:

from concourse.bass import DstId, RemoteDMATransfer
from concourse.mybir import AluOpType

NR, TK, DEG = 4, 128, 4
WC = TK * DEG
XH = TK // 2
HC = WC // 2

SCRATCH = {
    "x0": ("dram", [128, XH], "bfloat16"),
    "x1": ("dram", [128, TK - XH], "bfloat16"),
    "wl": ("dram", [128, HC], "bfloat16"),
    "wh": ("dram", [128, WC - HC], "bfloat16"),
    "xs": ("sbuf", [128, NR * TK], "bfloat16"),
    "ws": ("sbuf", [128, NR * WC], "bfloat16"),
    "hs": ("sbuf", [128, NR * TK], "bfloat16"),
    "ys": ("sbuf", [128, TK], "bfloat16"),
    "zero": ("sbuf", [128, TK], "float32"),
    "p0": ("psum", [128, 512], "float32"),
    "p1": ("psum", [128, 512], "float32"),
    "p2": ("psum", [128, 512], "float32"),
    "p3": ("psum", [128, 512], "float32"),
    "p4": ("psum", [128, 512], "float32"),
}
SEMAPHORES = (["lx", "lw", "ox", "ow", "xa", "wa", "sent", "zs", "st", "m4", "v4"]
              + ["ax%d" % j for j in range(NR)] + ["aw%d" % j for j in range(NR)]
              + ["al%d" % j for j in range(NR)] + ["ah%d" % j for j in range(NR)]
              + ["m%d" % j for j in range(NR)] + ["v%d" % j for j in range(NR)])

NX = 2
NH = 4
NF = 8
NN = 16


def _pick(mask, n, skip=0, step=1):
    bits = [1 << b for b in range(mask.bit_length()) if (mask >> b) & 1]
    m = 0
    for b in bits[skip:skip + n * step:step]:
        m |= b
    return m


def _plan(T, topo):
    cores = list(T.cores)
    every = range(topo.CORES_PER_CHIP * topo.CHIPS)
    near, far, pa, pc, jobs = {}, {}, {}, {}, {}
    for r, c in enumerate(cores):
        near[r] = [s for s, d in enumerate(cores) if s != r and topo.chip(d) == topo.chip(c)]
        f = [s for s, d in enumerate(cores) if topo.chip(d) != topo.chip(c)]
        far[r] = sorted(f, key=lambda s: (topo.die(cores[s]) != topo.die(c), s))
        fit = [p for p in every if topo.die(p) == topo.die(c) and p not in cores
               and all(topo.may_write(p, cores[s]) for s in f)]
        pa[r] = [p for p in fit if topo.chip(p) == topo.chip(c)][:len(f)]
        pc[r] = [p for p in fit if topo.same_plane(topo.chip(p), topo.chip(c)) and topo.may_write(c, p)
                 and all(topo.mates(topo.chip(p), topo.chip(cores[s])) for s in f)][:len(f)]
        for k, s in enumerate(far[r]):
            jobs[pa[r][k]] = ("a", r, s)
            jobs[pc[r][k]] = ("c", r, s)
    return cores, near, far, pa, pc, jobs


def _dst(topo, c):
    rid, pid, _ = topo.addr(c)
    return DstId(rid=rid, pnc=pid)


def _forward(g, core, T, topo, cores, job):
    way, r, s = job
    sem = T.sem
    rid, pid, _ = topo.addr(cores[s])
    m = _pick(topo.mask(core, cores[s]), NF)
    g.wait_ge(sem.xa, NX)
    if way == "a":
        g.remote_dma(T.xs[:, r * TK:r * TK + XH], T.x0[:], sem["ax%d" % r], sem.sent, pid, rid, m)
        g.wait_ge(sem.wa, NH)
        g.remote_dma(T.ws[:, r * WC:r * WC + HC], T.wl[:], sem["al%d" % r], sem.sent, pid, rid, m)
    else:
        g.remote_dma(T.xs[:, r * TK + XH:(r + 1) * TK], T.x1[:], sem["ax%d" % r], sem.sent, pid, rid, m)
        g.wait_ge(sem.wa, NH)
        g.remote_dma(T.ws[:, r * WC + HC:(r + 1) * WC], T.wh[:], sem["ah%d" % r], sem.sent, pid, rid, m)
    g.wait_ge(sem.sent, 2 * NF)


def _rank(g, core, T, topo, r, cores, near, far, pa, pc):
    sem = T.sem
    mask_tab = T.tables["MASK"]

    def xs(j):
        return T.xs[:, j * TK:(j + 1) * TK]

    def wall(j):
        return T.ws[:, j * WC:(j + 1) * WC]

    def wt(j, i):
        return T.ws[:, j * WC + i * TK:j * WC + (i + 1) * TK]

    def hs(j):
        return T.hs[:, j * TK:(j + 1) * TK]

    g.sync.dma_start(T.x0[:], T.x[:, 0:XH]).then_inc(sem.lx, 16)
    g.scalar.dma_start(T.x1[:], T.x[:, XH:TK]).then_inc(sem.lx, 16)
    g.sync.dma_start(T.wh[:], T.w[:, HC:WC]).then_inc(sem.lw, 16)
    g.scalar.dma_start(T.wl[:], T.w[:, 0:HC]).then_inc(sem.lw, 16)
    g.sync.dma_start(wall(r), T.w[:]).then_inc(sem.ow, 16)
    g.scalar.dma_start(xs(r), T.x[:]).then_inc(sem.ox, 16)
    g.vector.memset(T.zero[:], 0.0).then_inc(sem.zs, 1)

    out = topo.mask(core, pc[r][0])
    stay = topo.mask(core, pa[r][0]) & ~out

    def spread(jobs):
        g.remote_dma_fused(
            [RemoteDMATransfer(dst_ids=[_dst(topo, p)], dma_engine_mask=m, remote_sem=arrived, src=src[:], dst=src[:])
             for src, p, m, arrived in jobs],
            local_sem=sem.sent)
        return sum(bin(m).count("1") for _, _, m, _ in jobs)

    g.wait_ge(sem.lx, 32)
    sent = spread([(T.x1, p, _pick(out, NX, k * NH, NH // NX), sem.xa) for k, p in enumerate(pc[r])]
                  + [(T.x0, p, _pick(stay, NX, k * NH), sem.xa) for k, p in enumerate(pa[r])])
    g.wait_ge(sem.lw, 32)
    sent += spread([(T.wh, p, _pick(out, NH, k * NH), sem.wa) for k, p in enumerate(pc[r])]
                   + [(T.wl, p, _pick(stay, NH, k * NH), sem.wa) for k, p in enumerate(pa[r])])
    g.wait_ge(sem.ox, 16)
    g.wait_ge(sem.ow, 16)
    for s in near[r]:
        rid, pid, _ = topo.addr(cores[s])
        m = _pick(topo.mask(core, cores[s]), NN)
        g.remote_dma(xs(r), xs(r), sem["ax%d" % r], sem.sent, pid, rid, m)
        g.remote_dma(wall(r), wall(r), sem["aw%d" % r], sem.sent, pid, rid, m)
        sent += 2 * NN
    g.wait_ge(sem.sent, sent)

    here = [r] + near[r]
    order = here + far[r]
    pos = {j: k for k, j in enumerate(order)}
    waited = set()

    def need(name, val):
        if name not in waited:
            waited.add(name)
            g.tensor.wait_ge(sem[name], val)

    def need_x(j):
        if j == r:
            need("ox", 16)
        else:
            need("ax%d" % j, NN if j in near[r] else 2 * NF)

    def need_w(j, i):
        if j == r:
            need("ow", 16)
        elif j in near[r]:
            need("aw%d" % j, NN)
        else:
            if i * TK < HC:
                need("al%d" % j, NF)
            if (i + 1) * TK > HC:
                need("ah%d" % j, NF)

    done = {}

    def mm(grp, bank, total, lhsT, rhs):
        k = done.get(grp, 0)
        done[grp] = k + 1
        ins = g.tensor.matmul(bank[:, 0:TK], lhsT, rhs, k == 0, k + 1 == total)
        if k + 1 == total:
            ins.then_inc(sem["m%d" % grp], 1)

    def first(j, srcs, tiles):
        for i, s in sorted(enumerate(mask_tab[j]), key=lambda t: pos[t[1]]):
            if s in srcs and i in tiles:
                need_w(j, i)
                need_x(s)
                mm(j, T["p%d" % j], len(mask_tab[j]), wt(j, i), xs(s))

    def second(srcs):
        for i, s in sorted(enumerate(mask_tab[r]), key=lambda t: pos[t[1]]):
            if s in srcs:
                need("v%d" % s, 1)
                mm(NR, T.p4, len(mask_tab[r]), wt(r, i), hs(s))

    tiles = list(range(DEG))
    low = [i for i in tiles if (i + 1) * TK <= HC]
    high = [i for i in tiles if (i + 1) * TK > HC]
    for j in here:
        first(j, here, tiles)
    for j in here:
        first(j, far[r], tiles)
    for part in (low, high):
        for j in far[r]:
            first(j, order, part)
    second(order)

    g.vector.wait_ge(sem.zs, 1)
    for j in order:
        g.vector.wait_ge(sem["m%d" % j], 1)
        g.vector.tensor_tensor(hs(j), T["p%d" % j][:, 0:TK], T.zero[:], AluOpType.max).then_inc(sem["v%d" % j], 1)
    g.vector.wait_ge(sem.m4, 1)
    g.vector.tensor_tensor(T.ys[:], T.p4[:, 0:TK], T.zero[:], AluOpType.max).then_inc(sem.v4, 1)

    g.sync.wait_ge(sem.v4, 1)
    g.sync.dma_start(T.y[:], T.ys[:]).then_inc(sem.st, 16)
    g.sync.wait_ge(sem.st, 16)


def rank_program(g, core, T, topo):
    cores, near, far, pa, pc, jobs = _plan(T, topo)
    r = T.rank_of(core)
    if r is not None:
        _rank(g, core, T, topo, r, cores, near, far, pa, pc)
    elif core in jobs:
        _forward(g, core, T, topo, cores, jobs[core])
